import numpy as np
import ml_dtypes


def mxq(x, axis, fmt="e4m3"):
    dtype, down = {"e4m3": (ml_dtypes.float8_e4m3fn, 7), "e5m2": (ml_dtypes.float8_e5m2, 14)}[fmt]
    v = np.moveaxis(np.asarray(x, np.float32).astype(ml_dtypes.bfloat16).astype(np.float64), axis, -1)
    blocks = v.reshape(v.shape[:-1] + (-1, 32))
    amax = np.abs(blocks).max(-1, keepdims=True)
    byte = np.maximum(np.where(amax > 0, np.frexp(amax)[1] - 1 + 127, 0) - down, 1)
    scale = np.exp2(byte - 127.0)
    codes = (blocks / scale).astype(np.float32).astype(dtype).astype(np.float64)
    return np.moveaxis((codes * scale).reshape(v.shape), -1, axis)


WIDE = False


def mx_kscale(k):
    if not WIDE:
        return np.ones(k)
    levels = np.array([10, -10, 5, -5, 0])
    if k % 512:
        return np.exp2(np.random.permutation(np.resize(levels, k // 32))).repeat(32)
    a = np.empty((k // 512, 16))
    for p in range(k // 512):
        a[p, :8] = np.random.permutation(np.resize(levels, 8))
        for g in range(8):
            far = levels[np.abs(levels - a[p, g]) >= 10]
            a[p, g + 8] = far[np.random.randint(len(far))]
    return np.exp2(a.ravel()).repeat(32)


def f64(x):
    return np.asarray(x).astype(np.float64)


def striped(idx):
    return np.tile(idx.reshape(-1, 16).T, (8, 1)).astype(np.uint16)


def unstriped(offs):
    return offs[:16].T.reshape(-1).astype(np.int64)


def striped8(idx):
    return np.concatenate([x.reshape(-1, 16).T for x in idx]).astype(np.uint16)


def runs(offs, k):
    lists = np.stack([offs[16 * r : 16 * r + 16].T.reshape(-1) for r in range(8)]).astype(np.int64)
    return lists[np.arange(k) % 512 // 64]


def pack_weight(w):
    k, n = w.shape
    w = f64(np.asarray(w, np.float32).astype(ml_dtypes.bfloat16)).reshape(k // 32, 32, n)
    amax = np.abs(w).max(1)
    byte = np.clip(np.where(amax > 0, np.frexp(amax)[1] - 1 + 127 - 7, 1), 1, 254)
    scaled = (w * np.exp2(127.0 - byte)[:, None, :]).reshape(k, n).astype(np.float32)
    words = np.ascontiguousarray(scaled.reshape(k // 512, 128, 4, n).transpose(0, 1, 3, 2)).astype(ml_dtypes.float8_e4m3fn).view(np.uint8)
    return words, np.ascontiguousarray(byte.astype(np.uint8).reshape(k // 512, 16, n))


def unpack_weight(words, scales):
    g, p, n, _ = words.shape
    vals = np.ascontiguousarray(words).view(ml_dtypes.float8_e4m3fn).astype(np.float64) * np.repeat(np.exp2(scales.astype(np.float64) - 127.0), 8, axis=1)[..., None]
    return vals.transpose(0, 1, 3, 2).reshape(g * 512, n)


K, T, S, V, N, H, U = 512, 2048, 1024, 512, 512, 512, 1024


def setup_inputs():
    n = np.random.standard_normal
    s = mx_kscale(K)[:, None]
    u = mx_kscale(H)
    packed_xT = pack_weight(n((K, T)) * s)
    return {
        "x_words": packed_xT[0],
        "x_scales": packed_xT[1],
        "w1": (n((K, H)) / np.sqrt(K) / s * u).astype(np.float32),
        "w2": (n((H, H)) / np.sqrt(H) / u[:, None] * u).astype(np.float32),
        "mem": (n((H, U)) * u[:, None]).astype(np.float32),
        "w3": (n((H, N)) / np.sqrt(H) / u[:, None]).astype(np.float32),
        "res": n((N, U)).astype(np.float32),
        "offs": striped(np.random.permutation(T)[:S]),
        "n1": striped8(np.stack([np.random.permutation(S) for _ in range(8)])),
        "n2": striped8(np.stack([np.random.permutation(U)[:V] for _ in range(8)])),
    }


def reference(x_words, x_scales, w1, w2, mem, w3, res, offs, n1, n2):
    xq = unpack_weight(x_words, x_scales)[:, unstriped(offs)]
    y = mxq(f64(w1), 0, "e4m3").T @ xq
    ln = y[np.arange(H)[:, None], runs(n1, H)]
    z = ln.reshape(H, V, 2).max(axis=2)
    h = mxq(f64(w2), 0, "e4m3").T @ mxq(z, 0, "e4m3")
    z2 = f64(mem).copy()
    z2[np.arange(H)[:, None], runs(n2, H)] = h
    return f64(res) + (mxq(f64(w3), 0, "e4m3").T @ mxq(z2, 0, "e4m3"))

@@ -1,0 +1,194 @@
+from contextlib import ExitStack
+
+import concourse.mybir as mybir
+
+K, T, S, V, N, H, U = 512, 2048, 1024, 512, 512, 512, 1024
+FLOPS = 2 * K * H * S + 2 * H * H * V + 2 * H * N * U
+
+F32 = mybir.dt.float32
+BF16 = mybir.dt.bfloat16
+I32 = mybir.dt.int32
+U32 = mybir.dt.uint32
+U16 = mybir.dt.uint16
+U8 = mybir.dt.uint8
+FP8X4 = mybir.dt.float8_e4m3fn_x4
+ADD = mybir.AluOpType.add
+MAX = mybir.AluOpType.max
+
+P = 128
+PACK = 4
+BANK = 512
+ALIGN = 64
+LIST_ROWS = 16
+HALF = 512
+POOLED = HALF // 2
+PAGE_CHUNKS = (128, 256, 256, 256, 128)
+
+
+def deal_weights(copy, grouped, raw, first, count, raw_first):
+    copy(
+        out=grouped[:, :, first : first + count, :].rearrange("p t m j -> p m j t"),
+        in_=raw[:, :, raw_first : raw_first + PACK * count].rearrange("p j (m t) -> p m j t", t=PACK),
+    )
+
+
+def tile_picked_deeppoolpage_none_p_kernel(
+    tc, x_words, x_scales, w1, w2, mem, w3, res, offs, n1, n2, out
+):
+    nc = tc.nc
+    with ExitStack() as ctx:
+        keep = ctx.enter_context(tc.tile_pool(name="keep", bufs=1))
+        psum = ctx.enter_context(tc.psum_pool(name="psum", bufs=8))
+
+        def bank(shape):
+            return psum.tile(shape, F32, name="bank", tag="bank")
+
+        def quantize(codes, scales, values):
+            nc.vector.quantize_mx(out=codes.bitcast(FP8X4), scales=scales, in_=values)
+
+        def product(acc, w_codes, w_scales, t, codes, scales):
+            nc.tensor.matmul_mx(
+                out=acc,
+                lhsT=w_codes[:, t * P : (t + 1) * P].bitcast(FP8X4),
+                lhsT_scale=w_scales[:, t * P : (t + 1) * P],
+                rhs=codes.bitcast(FP8X4),
+                rhs_scale=scales,
+                start=True,
+                stop=True,
+            )
+
+        offs_sb = keep.tile([P, S // LIST_ROWS], U16, name="offs_sb")
+        n1_sb = keep.tile([P, S // LIST_ROWS], U16, name="n1_sb")
+        n2_sb = keep.tile([P, V // LIST_ROWS], U16, name="n2_sb")
+        words_all = keep.tile([P, T], U32, name="words_all")
+        scales_all = keep.tile([P, T], U8, name="scales_all")
+        nc.sync.dma_start(offs_sb[:], offs)
+        for q in range(4):
+            nc.sync.dma_start(
+                scales_all[32 * q : 32 * q + 32, :].bitcast(I32),
+                x_scales[0:1, 4 * q : 4 * q + 4, :].bitcast(I32).to_broadcast([8, 4, T // 4]),
+            )
+        nc.sync.dma_start(words_all[:].bitcast(I32), x_words[0].rearrange("p n j -> p (n j)").bitcast(I32))
+        w1_rows = w1.rearrange("(p j) c -> p j c", j=PACK)
+        w1_raw = [keep.tile([P, PACK, H // 2], F32, name=f"w1_raw{a}") for a in range(2)]
+        for a in range(2):
+            nc.sync.dma_start(w1_raw[a][:], w1_rows[:, :, a * (H // 2) : (a + 1) * (H // 2)])
+        nc.sync.dma_start(n1_sb[:], n1)
+        w2_raw = keep.tile([P, PACK, H], F32, name="w2_raw")
+        nc.sync.dma_start(w2_raw[:], w2.rearrange("(p j) c -> p j c", j=PACK))
+        w3_raw = keep.tile([P, PACK, N], F32, name="w3_raw")
+        nc.sync.dma_start(w3_raw[:], w3.rearrange("(p j) c -> p j c", j=PACK))
+        nc.sync.dma_start(n2_sb[:], n2)
+        mem_rows = mem.rearrange("(p t) w -> t p w", t=PACK)
+        page = [keep.tile([P, U * (2 - t % 2)], F32, name=f"page{t}") for t in range(PACK)]
+        for t in (1, 3, 0, 2):
+            nc.sync.dma_start(page[t][:, :U], mem_rows[t])
+        res_sb = keep.tile([P, PACK, U], F32, name="res_sb")
+        nc.sync.dma_start(res_sb[:], res.rearrange("(p t) w -> p t w", t=PACK))
+
+        x_scale = keep.tile([P, S], U8, name="x_scale", align_bytes=ALIGN)
+        nc.vector.tensor_copy(x_scale[:], scales_all[:].indirect(offs_sb[:]))
+        x_codes = []
+        cols = HALF // LIST_ROWS
+        for a in range(2):
+            picked = keep.tile([P, HALF], U32, name=f"x_codes{a}", align_bytes=ALIGN)
+            nc.vector.tensor_copy(picked[:], words_all[:].indirect(offs_sb[:, a * cols : (a + 1) * cols]))
+            x_codes.append(picked)
+
+        w1_grouped = keep.tile([P, PACK, P, PACK], BF16, name="w1_grouped", align_bytes=ALIGN)
+        deal_weights(nc.scalar.copy, w1_grouped, w1_raw[0], 0, 64, 0)
+        deal_weights(nc.scalar.copy, w1_grouped, w1_raw[1], 64, 32, 0)
+        deal_weights(nc.vector.tensor_copy, w1_grouped, w1_raw[1], 96, 32, 128)
+        w1_codes = keep.tile([P, H], U32, name="w1_codes", tag="chain", align_bytes=ALIGN)
+        w1_scale = keep.tile([P, H], U8, name="w1_scale", align_bytes=ALIGN)
+        for t in range(PACK):
+            quantize(
+                w1_codes[:, t * P : (t + 1) * P],
+                w1_scale[:, t * P : (t + 1) * P],
+                w1_grouped[:, t].rearrange("p m j -> p (m j)"),
+            )
+
+        y = [keep.tile([P, S], F32, name=f"y{t}") for t in range(PACK)]
+        for t in range(PACK):
+            for a in range(2):
+                acc = bank([P, HALF])
+                product(acc[:], w1_codes, w1_scale, t, x_codes[a][:], x_scale[:, a * HALF : (a + 1) * HALF])
+                copy = nc.vector.tensor_copy if (t, a) == (0, 1) else nc.scalar.copy
+                copy(out=y[t][:, a * HALF : (a + 1) * HALF], in_=acc[:])
+
+        w2_grouped = keep.tile([P, PACK, P, PACK], BF16, name="w2_grouped", tag="chain", align_bytes=ALIGN)
+        deal_weights(nc.scalar.copy, w2_grouped, w2_raw, 0, P, 0)
+        w3_grouped = keep.tile([P, PACK, P, PACK], BF16, name="w3_grouped", align_bytes=ALIGN)
+        deal_weights(nc.scalar.copy, w3_grouped, w3_raw, 0, P, 0)
+
+        lined = [keep.tile([P, PACK, HALF], F32, name=f"lined{c}") for c in range(2)]
+        for t in range(PACK):
+            for c in range(2):
+                nc.vector.tensor_copy(lined[c][:, t, :], y[t][:].indirect(n1_sb[:, c * cols : (c + 1) * cols]))
+
+        w2_codes = keep.tile([P, H], U32, name="w2_codes", align_bytes=ALIGN)
+        w2_scale = keep.tile([P, H], U8, name="w2_scale", align_bytes=ALIGN)
+        quantize(w2_codes[:], w2_scale[:], w2_grouped[:].rearrange("p t m j -> p (t m j)"))
+
+        h = [keep.tile([P, V], F32, name=f"h{t}") for t in range(PACK)]
+        slot_cols = POOLED // LIST_ROWS
+        for c in range(2):
+            z_grouped = keep.tile(
+                [P, POOLED, PACK], BF16, name=f"z_grouped{c}", tag=("chain" if c == 0 else "z_second"), align_bytes=ALIGN
+            )
+            pairs = lined[c][:].rearrange("p t (v i e) -> p e v t i", i=4, e=2)
+            nc.vector.tensor_tensor(
+                z_grouped[:].rearrange("p (v i) t -> p v t i", i=4), pairs[:, 0], pairs[:, 1], MAX
+            )
+            z_codes = keep.tile([P, POOLED], U32, name=f"z_codes{c}", align_bytes=ALIGN)
+            z_scale = keep.tile([P, POOLED], U8, name=f"z_scale{c}", align_bytes=ALIGN)
+            quantize(z_codes[:], z_scale[:], z_grouped[:].rearrange("p v t -> p (v t)"))
+            for t in (1, 3, 0, 2):
+                acc = bank([P, POOLED])
+                product(acc[:], w2_codes, w2_scale, t, z_codes[:], z_scale[:])
+                nc.scalar.copy(out=h[t][:, c * POOLED : (c + 1) * POOLED], in_=acc[:])
+
+        w3_codes = keep.tile([P, N], U32, name="w3_codes", align_bytes=ALIGN)
+        w3_scale = keep.tile([P, N], U8, name="w3_scale", align_bytes=ALIGN)
+        quantize(w3_codes[:], w3_scale[:], w3_grouped[:].rearrange("p t m j -> p (t m j)"))
+
+        for c in range(2):
+            for t in (1, 3):
+                nc.vector.tensor_copy(
+                    page[t][:].indirect(n2_sb[:, c * slot_cols : (c + 1) * slot_cols]),
+                    h[t][:, c * POOLED : (c + 1) * POOLED],
+                )
+        for t in (1, 3):
+            nc.scalar.copy(out=page[t - 1][:, U:], in_=page[t][:])
+        starts = [sum(PAGE_CHUNKS[:c]) for c in range(len(PAGE_CHUNKS))]
+        z2_grouped = [
+            keep.tile([P, width, PACK], BF16, name=f"z2_grouped{c}", align_bytes=ALIGN)
+            for c, width in enumerate(PAGE_CHUNKS)
+        ]
+
+        def weave(copy, c, t):
+            both = page[t][:].rearrange("p (e w) -> p w e", e=2)[:, starts[c] : starts[c] + PAGE_CHUNKS[c], :]
+            copy(out=z2_grouped[c][:, :, t : t + 2], in_=both)
+
+        nc.vector.tensor_copy(page[0][:].indirect(n2_sb[:]), h[0][:])
+        for c in range(len(PAGE_CHUNKS)):
+            weave(nc.scalar.copy, c, 0)
+        nc.vector.tensor_copy(page[2][:].indirect(n2_sb[:]), h[2][:])
+
+        out_rows = out.rearrange("(p t) w -> p t w", t=PACK)
+        for c, width in enumerate(PAGE_CHUNKS):
+            weave(nc.vector.tensor_copy if c == 0 else nc.scalar.copy, c, 2)
+            z2_codes = keep.tile([P, width], U32, name=f"z2_codes{c}", align_bytes=ALIGN)
+            z2_scale = keep.tile([P, width], U8, name=f"z2_scale{c}", align_bytes=ALIGN)
+            quantize(z2_codes[:], z2_scale[:], z2_grouped[c][:].rearrange("p w t -> p (w t)"))
+            result = keep.tile([P, PACK, width], F32, name=f"result{c}")
+            per_bank = BANK // width
+            columns = slice(starts[c], starts[c] + width)
+            for first in range(0, PACK, per_bank):
+                acc = bank([P, per_bank, width])
+                for t in range(first, first + per_bank):
+                    product(acc[:, t - first, :], w3_codes, w3_scale, t, z2_codes[:], z2_scale[:])
+                nc.vector.tensor_tensor(
+                    result[:, first : first + per_bank, :], acc[:], res_sb[:, first : first + per_bank, columns], ADD
+                )
+            nc.sync.dma_start(out_rows[:, :, columns], result[:])

@@ -25,11 +25,15 @@ POOLED = HALF // 2
 PAGE_CHUNKS = (128, 256, 256, 256, 128)
 
 
-def deal_weights(copy, grouped, raw, first, count, raw_first):
-    copy(
-        out=grouped[:, :, first : first + count, :].rearrange("p t m j -> p m j t"),
-        in_=raw[:, :, raw_first : raw_first + PACK * count].rearrange("p j (m t) -> p m j t", t=PACK),
+def deal_weights(nc, grouped, raw, tiles, blocks):
+    nc.scalar.copy(
+        out=grouped[:, tiles, 8 * blocks.start : 8 * blocks.stop, :].rearrange("p t (a b) j -> p t a b j", b=8),
+        in_=raw[:].rearrange("p j (a t b) -> p t a b j", t=PACK, b=8)[:, tiles],
     )
+
+
+def dealt_rows(rows, t):
+    return rows.rearrange("(a t b) c -> t a b c", t=PACK, b=8)[t]
 
 
 def tile_picked_deeppoolpage_none_p_kernel(
@@ -75,16 +79,17 @@ def tile_picked_deeppoolpage_none_p_kernel(
             nc.sync.dma_start(w1_raw[a][:], w1_rows[:, :, a * (H // 2) : (a + 1) * (H // 2)])
         nc.sync.dma_start(n1_sb[:], n1)
         w2_raw = keep.tile([P, PACK, H], F32, name="w2_raw")
-        nc.sync.dma_start(w2_raw[:], w2.rearrange("(p j) c -> p j c", j=PACK))
+        for t in range(PACK):
+            nc.sync.dma_start(w2_raw[:, t, :], dealt_rows(w2, t))
         w3_raw = keep.tile([P, PACK, N], F32, name="w3_raw")
-        nc.sync.dma_start(w3_raw[:], w3.rearrange("(p j) c -> p j c", j=PACK))
+        for t in range(PACK):
+            nc.sync.dma_start(w3_raw[:, t, :], dealt_rows(w3, t))
         nc.sync.dma_start(n2_sb[:], n2)
-        mem_rows = mem.rearrange("(p t) w -> t p w", t=PACK)
         page = [keep.tile([P, U * (2 - t % 2)], F32, name=f"page{t}") for t in range(PACK)]
         for t in (1, 3, 0, 2):
-            nc.sync.dma_start(page[t][:, :U], mem_rows[t])
+            nc.sync.dma_start(page[t][:, :U], dealt_rows(mem, t))
         res_sb = keep.tile([P, PACK, U], F32, name="res_sb")
-        nc.sync.dma_start(res_sb[:], res.rearrange("(p t) w -> p t w", t=PACK))
+        nc.sync.dma_start(res_sb[:], res.rearrange("(t p) w -> p t w", t=PACK))
 
         x_scale = keep.tile([P, S], U8, name="x_scale", align_bytes=ALIGN)
         nc.vector.tensor_copy(x_scale[:], scales_all[:].indirect(offs_sb[:]))
@@ -96,9 +101,9 @@ def tile_picked_deeppoolpage_none_p_kernel(
             x_codes.append(picked)
 
         w1_grouped = keep.tile([P, PACK, P, PACK], BF16, name="w1_grouped", align_bytes=ALIGN)
-        deal_weights(nc.scalar.copy, w1_grouped, w1_raw[0], 0, 64, 0)
-        deal_weights(nc.scalar.copy, w1_grouped, w1_raw[1], 64, 32, 0)
-        deal_weights(nc.vector.tensor_copy, w1_grouped, w1_raw[1], 96, 32, 128)
+        deal_weights(nc, w1_grouped, w1_raw[0], slice(0, PACK), range(0, 8))
+        for t in range(PACK):
+            deal_weights(nc, w1_grouped, w1_raw[1], slice(t, t + 1), range(8, 16))
         w1_codes = keep.tile([P, H], U32, name="w1_codes", tag="chain", align_bytes=ALIGN)
         w1_scale = keep.tile([P, H], U8, name="w1_scale", align_bytes=ALIGN)
         for t in range(PACK):
@@ -117,14 +122,18 @@ def tile_picked_deeppoolpage_none_p_kernel(
                 copy(out=y[t][:, a * HALF : (a + 1) * HALF], in_=acc[:])
 
         w2_grouped = keep.tile([P, PACK, P, PACK], BF16, name="w2_grouped", tag="chain", align_bytes=ALIGN)
-        deal_weights(nc.scalar.copy, w2_grouped, w2_raw, 0, P, 0)
-        w3_grouped = keep.tile([P, PACK, P, PACK], BF16, name="w3_grouped", align_bytes=ALIGN)
-        deal_weights(nc.scalar.copy, w3_grouped, w3_raw, 0, P, 0)
+        deal_weights(nc, w2_grouped, w2_raw, slice(0, PACK), range(0, 16))
+        w3_grouped = keep.tile([P, N, PACK], BF16, name="w3_grouped", align_bytes=ALIGN)
+        nc.scalar.copy(out=w3_grouped[:], in_=w3_raw[:].rearrange("p j c -> p c j"))
 
-        lined = [keep.tile([P, PACK, HALF], F32, name=f"lined{c}") for c in range(2)]
+        z = [keep.tile([P, PACK, POOLED], BF16, name=f"z{c}") for c in range(2)]
         for t in range(PACK):
+            lined = [keep.tile([P, HALF], F32, name=f"lined{t}_{c}") for c in range(2)]
             for c in range(2):
-                nc.vector.tensor_copy(lined[c][:, t, :], y[t][:].indirect(n1_sb[:, c * cols : (c + 1) * cols]))
+                nc.vector.tensor_copy(lined[c][:], y[t][:].indirect(n1_sb[:, c * cols : (c + 1) * cols]))
+            for c in range(2):
+                pairs = lined[c][:].rearrange("p (v e) -> p e v", e=2)
+                nc.vector.tensor_tensor(z[c][:, t, :], pairs[:, 0], pairs[:, 1], MAX)
 
         w2_codes = keep.tile([P, H], U32, name="w2_codes", align_bytes=ALIGN)
         w2_scale = keep.tile([P, H], U8, name="w2_scale", align_bytes=ALIGN)
@@ -132,17 +141,15 @@ def tile_picked_deeppoolpage_none_p_kernel(
 
         h = [keep.tile([P, V], F32, name=f"h{t}") for t in range(PACK)]
         slot_cols = POOLED // LIST_ROWS
+        z_grouped = [keep.tile([P, POOLED, PACK], BF16, name=f"z_grouped{c}", align_bytes=ALIGN) for c in range(2)]
+        nc.vector.tensor_copy(out=z_grouped[0][:], in_=z[0][:].rearrange("p t v -> p v t"))
+        nc.scalar.copy(out=z_grouped[1][:], in_=z[1][:].rearrange("p t v -> p v t"))
         for c in range(2):
-            z_grouped = keep.tile(
-                [P, POOLED, PACK], BF16, name=f"z_grouped{c}", tag=("chain" if c == 0 else "z_second"), align_bytes=ALIGN
+            z_codes = keep.tile(
+                [P, POOLED], U32, name=f"z_codes{c}", tag=("chain" if c == 0 else "z_second"), align_bytes=ALIGN
             )
-            pairs = lined[c][:].rearrange("p t (v i e) -> p e v t i", i=4, e=2)
-            nc.vector.tensor_tensor(
-                z_grouped[:].rearrange("p (v i) t -> p v t i", i=4), pairs[:, 0], pairs[:, 1], MAX
-            )
-            z_codes = keep.tile([P, POOLED], U32, name=f"z_codes{c}", align_bytes=ALIGN)
             z_scale = keep.tile([P, POOLED], U8, name=f"z_scale{c}", align_bytes=ALIGN)
-            quantize(z_codes[:], z_scale[:], z_grouped[:].rearrange("p v t -> p (v t)"))
+            quantize(z_codes[:], z_scale[:], z_grouped[c][:].rearrange("p v t -> p (v t)"))
             for t in (1, 3, 0, 2):
                 acc = bank([P, POOLED])
                 product(acc[:], w2_codes, w2_scale, t, z_codes[:], z_scale[:])
@@ -150,7 +157,7 @@ def tile_picked_deeppoolpage_none_p_kernel(
 
         w3_codes = keep.tile([P, N], U32, name="w3_codes", align_bytes=ALIGN)
         w3_scale = keep.tile([P, N], U8, name="w3_scale", align_bytes=ALIGN)
-        quantize(w3_codes[:], w3_scale[:], w3_grouped[:].rearrange("p t m j -> p (t m j)"))
+        quantize(w3_codes[:], w3_scale[:], w3_grouped[:].rearrange("p c j -> p (c j)"))
 
         for c in range(2):
             for t in (1, 3):
@@ -175,7 +182,7 @@ def tile_picked_deeppoolpage_none_p_kernel(
             weave(nc.scalar.copy, c, 0)
         nc.vector.tensor_copy(page[2][:].indirect(n2_sb[:]), h[2][:])
 
-        out_rows = out.rearrange("(p t) w -> p t w", t=PACK)
+        out_rows = out.rearrange("(t p) w -> p t w", t=PACK)
         for c, width in enumerate(PAGE_CHUNKS):
             weave(nc.vector.tensor_copy if c == 0 else nc.scalar.copy, c, 2)
             z2_codes = keep.tile([P, width], U32, name=f"z2_codes{c}", align_bytes=ALIGN)

@@ -21,13 +21,14 @@ BANK = 512
 ALIGN = 64
 LIST_ROWS = 16
 HALF = 512
+EARLY = 768
 POOLED = HALF // 2
-PAGE_CHUNKS = (128, 256, 256, 256, 128)
+PAGE_CHUNKS = (256, 256, 512)
 
 
 def deal_weights(nc, grouped, raw, tiles, blocks):
     nc.scalar.copy(
-        out=grouped[:, tiles, 8 * blocks.start : 8 * blocks.stop, :].rearrange("p t (a b) j -> p t a b j", b=8),
+        out=grouped[:, :, 8 * blocks.start : 8 * blocks.stop, :].rearrange("p t (a b) j -> p t a b j", b=8),
         in_=raw[:].rearrange("p j (a t b) -> p t a b j", t=PACK, b=8)[:, tiles],
     )
 
@@ -65,12 +66,12 @@ def tile_picked_deeppoolpage_none_p_kernel(
         n1_sb = keep.tile([P, S // LIST_ROWS], U16, name="n1_sb")
         n2_sb = keep.tile([P, V // LIST_ROWS], U16, name="n2_sb")
         words_all = keep.tile([P, T], U32, name="words_all")
-        scales_all = keep.tile([P, T], U8, name="scales_all")
+        scales_all = keep.tile([P, T], U8, name="scales_all", tag="scale_table", align_bytes=ALIGN)
         nc.sync.dma_start(offs_sb[:], offs)
+        nc.vector.memset(scales_all[:].bitcast(I32), 0)
         for q in range(4):
-            nc.sync.dma_start(
-                scales_all[32 * q : 32 * q + 32, :].bitcast(I32),
-                x_scales[0:1, 4 * q : 4 * q + 4, :].bitcast(I32).to_broadcast([8, 4, T // 4]),
+            nc.scalar.dma_start(
+                scales_all[32 * q : 32 * q + 4, :].bitcast(I32), x_scales[0, 4 * q : 4 * q + 4, :].bitcast(I32)
             )
         nc.sync.dma_start(words_all[:].bitcast(I32), x_words[0].rearrange("p n j -> p (n j)").bitcast(I32))
         w1_rows = w1.rearrange("(p j) c -> p j c", j=PACK)
@@ -93,42 +94,53 @@ def tile_picked_deeppoolpage_none_p_kernel(
 
         x_scale = keep.tile([P, S], U8, name="x_scale", align_bytes=ALIGN)
         nc.vector.tensor_copy(x_scale[:], scales_all[:].indirect(offs_sb[:]))
-        x_codes = []
         cols = HALF // LIST_ROWS
-        for a in range(2):
-            picked = keep.tile([P, HALF], U32, name=f"x_codes{a}", align_bytes=ALIGN)
-            nc.vector.tensor_copy(picked[:], words_all[:].indirect(offs_sb[:, a * cols : (a + 1) * cols]))
-            x_codes.append(picked)
+        early_codes = keep.tile([P, EARLY], U32, name="early_codes", tag="scale_table", align_bytes=ALIGN)
+        nc.vector.tensor_copy(early_codes[:], words_all[:].indirect(offs_sb[:, : EARLY // LIST_ROWS]))
 
-        w1_grouped = keep.tile([P, PACK, P, PACK], BF16, name="w1_grouped", align_bytes=ALIGN)
-        deal_weights(nc, w1_grouped, w1_raw[0], slice(0, PACK), range(0, 8))
-        for t in range(PACK):
-            deal_weights(nc, w1_grouped, w1_raw[1], slice(t, t + 1), range(8, 16))
+        w1_first = keep.tile([P, 1, P, PACK], BF16, name="w1_first", tag="w1_first", align_bytes=ALIGN)
+        w1_rest = keep.tile([P, PACK - 1, P, PACK], BF16, name="w1_rest", align_bytes=ALIGN)
+        deal_weights(nc, w1_first[:], w1_raw[0], slice(0, 1), range(0, 8))
+        deal_weights(nc, w1_rest[:], w1_raw[0], slice(1, PACK), range(0, 8))
+        deal_weights(nc, w1_first[:], w1_raw[1], slice(0, 1), range(8, 16))
+        for t in range(1, PACK):
+            deal_weights(nc, w1_rest[:, t - 1 : t], w1_raw[1], slice(t, t + 1), range(8, 16))
         w1_codes = keep.tile([P, H], U32, name="w1_codes", tag="chain", align_bytes=ALIGN)
         w1_scale = keep.tile([P, H], U8, name="w1_scale", align_bytes=ALIGN)
-        for t in range(PACK):
+        quantize(w1_codes[:, :P], w1_scale[:, :P], w1_first[:, 0].rearrange("p m j -> p (m j)"))
+        late_codes = keep.tile([P, S - EARLY], U32, name="late_codes", tag="w1_first", align_bytes=ALIGN)
+        nc.vector.tensor_copy(late_codes[:], words_all[:].indirect(offs_sb[:, EARLY // LIST_ROWS :]))
+        for t in range(1, PACK):
             quantize(
                 w1_codes[:, t * P : (t + 1) * P],
                 w1_scale[:, t * P : (t + 1) * P],
-                w1_grouped[:, t].rearrange("p m j -> p (m j)"),
+                w1_rest[:, t - 1].rearrange("p m j -> p (m j)"),
             )
 
         y = [keep.tile([P, S], F32, name=f"y{t}") for t in range(PACK)]
         for t in range(PACK):
-            for a in range(2):
+            acc = bank([P, HALF])
+            product(acc[:], w1_codes, w1_scale, t, early_codes[:, :HALF], x_scale[:, :HALF])
+            nc.scalar.copy(out=y[t][:, :HALF], in_=acc[:])
+            if t == 0:
+                for codes, first, last in ((early_codes[:, HALF:], HALF, EARLY), (late_codes[:], EARLY, S)):
+                    acc = bank([P, last - first])
+                    product(acc[:], w1_codes, w1_scale, t, codes, x_scale[:, first:last])
+                    nc.vector.tensor_copy(out=y[t][:, first:last], in_=acc[:])
+            else:
                 acc = bank([P, HALF])
-                product(acc[:], w1_codes, w1_scale, t, x_codes[a][:], x_scale[:, a * HALF : (a + 1) * HALF])
-                copy = nc.vector.tensor_copy if (t, a) == (0, 1) else nc.scalar.copy
-                copy(out=y[t][:, a * HALF : (a + 1) * HALF], in_=acc[:])
+                for codes, first, last in ((early_codes[:, HALF:], HALF, EARLY), (late_codes[:], EARLY, S)):
+                    product(acc[:, first - HALF : last - HALF], w1_codes, w1_scale, t, codes, x_scale[:, first:last])
+                nc.scalar.copy(out=y[t][:, HALF:], in_=acc[:])
 
         w2_grouped = keep.tile([P, PACK, P, PACK], BF16, name="w2_grouped", tag="chain", align_bytes=ALIGN)
-        deal_weights(nc, w2_grouped, w2_raw, slice(0, PACK), range(0, 16))
+        deal_weights(nc, w2_grouped[:], w2_raw, slice(0, PACK), range(0, 16))
         w3_grouped = keep.tile([P, N, PACK], BF16, name="w3_grouped", align_bytes=ALIGN)
         nc.scalar.copy(out=w3_grouped[:], in_=w3_raw[:].rearrange("p j c -> p c j"))
 
         z = [keep.tile([P, PACK, POOLED], BF16, name=f"z{c}") for c in range(2)]
         for t in range(PACK):
-            lined = [keep.tile([P, HALF], F32, name=f"lined{t}_{c}") for c in range(2)]
+            lined = [keep.tile([P, HALF], BF16, name=f"lined{t}_{c}") for c in range(2)]
             for c in range(2):
                 nc.vector.tensor_copy(lined[c][:], y[t][:].indirect(n1_sb[:, c * cols : (c + 1) * cols]))
             for c in range(2):
@@ -183,19 +195,22 @@ def tile_picked_deeppoolpage_none_p_kernel(
         nc.vector.tensor_copy(page[2][:].indirect(n2_sb[:]), h[2][:])
 
         out_rows = out.rearrange("(t p) w -> p t w", t=PACK)
+        z2_mx = []
         for c, width in enumerate(PAGE_CHUNKS):
             weave(nc.vector.tensor_copy if c == 0 else nc.scalar.copy, c, 2)
             z2_codes = keep.tile([P, width], U32, name=f"z2_codes{c}", align_bytes=ALIGN)
             z2_scale = keep.tile([P, width], U8, name=f"z2_scale{c}", align_bytes=ALIGN)
             quantize(z2_codes[:], z2_scale[:], z2_grouped[c][:].rearrange("p w t -> p (w t)"))
-            result = keep.tile([P, PACK, width], F32, name=f"result{c}")
+            z2_mx.append((z2_codes, z2_scale))
+        for c, width in enumerate(PAGE_CHUNKS):
+            z2_codes, z2_scale = z2_mx[c]
             per_bank = BANK // width
             columns = slice(starts[c], starts[c] + width)
             for first in range(0, PACK, per_bank):
                 acc = bank([P, per_bank, width])
                 for t in range(first, first + per_bank):
                     product(acc[:, t - first, :], w3_codes, w3_scale, t, z2_codes[:], z2_scale[:])
-                nc.vector.tensor_tensor(
-                    result[:, first : first + per_bank, :], acc[:], res_sb[:, first : first + per_bank, columns], ADD
-                )
-            nc.sync.dma_start(out_rows[:, :, columns], result[:])
+                rows = slice(first, first + per_bank)
+                result = keep.tile([P, per_bank, width], F32, name=f"result{c}_{first}")
+                nc.vector.tensor_tensor(result[:], acc[:], res_sb[:, rows, columns], ADD)
+                nc.sync.dma_start(out_rows[:, rows, columns], result[:])

from contextlib import ExitStack

import concourse.mybir as mybir

K, T, S, V, N, H, U = 512, 2048, 1024, 512, 512, 512, 1024
FLOPS = 2 * K * H * S + 2 * H * H * V + 2 * H * N * U

F32 = mybir.dt.float32
BF16 = mybir.dt.bfloat16
I32 = mybir.dt.int32
U32 = mybir.dt.uint32
U16 = mybir.dt.uint16
U8 = mybir.dt.uint8
FP8X4 = mybir.dt.float8_e4m3fn_x4
ADD = mybir.AluOpType.add
MAX = mybir.AluOpType.max

P = 128
PACK = 4
BANK = 512
ALIGN = 64
LIST_ROWS = 16
HALF = 512
EARLY = 768
POOLED = HALF // 2
PAGE_CHUNKS = (256, 256, 512)


def deal_weights(nc, grouped, raw, tiles, blocks):
    nc.scalar.copy(
        out=grouped[:, :, 8 * blocks.start : 8 * blocks.stop, :].rearrange("p t (a b) j -> p t a b j", b=8),
        in_=raw[:].rearrange("p j (a t b) -> p t a b j", t=PACK, b=8)[:, tiles],
    )


def dealt_rows(rows, t):
    return rows.rearrange("(a t b) c -> t a b c", t=PACK, b=8)[t]


def tile_picked_deeppoolpage_none_p_kernel(
    tc, x_words, x_scales, w1, w2, mem, w3, res, offs, n1, n2, out
):
    nc = tc.nc
    with ExitStack() as ctx:
        keep = ctx.enter_context(tc.tile_pool(name="keep", bufs=1))
        psum = ctx.enter_context(tc.psum_pool(name="psum", bufs=8))

        def bank(shape):
            return psum.tile(shape, F32, name="bank", tag="bank")

        def quantize(codes, scales, values):
            nc.vector.quantize_mx(out=codes.bitcast(FP8X4), scales=scales, in_=values)

        def product(acc, w_codes, w_scales, t, codes, scales):
            nc.tensor.matmul_mx(
                out=acc,
                lhsT=w_codes[:, t * P : (t + 1) * P].bitcast(FP8X4),
                lhsT_scale=w_scales[:, t * P : (t + 1) * P],
                rhs=codes.bitcast(FP8X4),
                rhs_scale=scales,
                start=True,
                stop=True,
            )

        offs_sb = keep.tile([P, S // LIST_ROWS], U16, name="offs_sb")
        n1_sb = keep.tile([P, S // LIST_ROWS], U16, name="n1_sb")
        n2_sb = keep.tile([P, V // LIST_ROWS], U16, name="n2_sb")
        words_all = keep.tile([P, T], U32, name="words_all")
        scales_all = keep.tile([P, T], U8, name="scales_all", tag="scale_table", align_bytes=ALIGN)
        nc.sync.dma_start(offs_sb[:], offs)
        nc.vector.memset(scales_all[:].bitcast(I32), 0)
        for q in range(4):
            nc.scalar.dma_start(
                scales_all[32 * q : 32 * q + 4, :].bitcast(I32), x_scales[0, 4 * q : 4 * q + 4, :].bitcast(I32)
            )
        nc.sync.dma_start(words_all[:].bitcast(I32), x_words[0].rearrange("p n j -> p (n j)").bitcast(I32))
        w1_rows = w1.rearrange("(p j) c -> p j c", j=PACK)
        w1_raw = [keep.tile([P, PACK, H // 2], F32, name=f"w1_raw{a}") for a in range(2)]
        for a in range(2):
            nc.sync.dma_start(w1_raw[a][:], w1_rows[:, :, a * (H // 2) : (a + 1) * (H // 2)])
        nc.sync.dma_start(n1_sb[:], n1)
        w2_raw = keep.tile([P, PACK, H], F32, name="w2_raw")
        for t in range(PACK):
            nc.sync.dma_start(w2_raw[:, t, :], dealt_rows(w2, t))
        w3_raw = keep.tile([P, PACK, N], F32, name="w3_raw")
        for t in range(PACK):
            nc.sync.dma_start(w3_raw[:, t, :], dealt_rows(w3, t))
        nc.sync.dma_start(n2_sb[:], n2)
        page = [keep.tile([P, U * (2 - t % 2)], F32, name=f"page{t}") for t in range(PACK)]
        for t in (1, 3, 0, 2):
            nc.sync.dma_start(page[t][:, :U], dealt_rows(mem, t))
        res_sb = keep.tile([P, PACK, U], F32, name="res_sb")
        nc.sync.dma_start(res_sb[:], res.rearrange("(t p) w -> p t w", t=PACK))

        x_scale = keep.tile([P, S], U8, name="x_scale", align_bytes=ALIGN)
        nc.vector.tensor_copy(x_scale[:], scales_all[:].indirect(offs_sb[:]))
        cols = HALF // LIST_ROWS
        early_codes = keep.tile([P, EARLY], U32, name="early_codes", tag="scale_table", align_bytes=ALIGN)
        nc.vector.tensor_copy(early_codes[:], words_all[:].indirect(offs_sb[:, : EARLY // LIST_ROWS]))

        w1_first = keep.tile([P, 1, P, PACK], BF16, name="w1_first", tag="w1_first", align_bytes=ALIGN)
        w1_rest = keep.tile([P, PACK - 1, P, PACK], BF16, name="w1_rest", align_bytes=ALIGN)
        deal_weights(nc, w1_first[:], w1_raw[0], slice(0, 1), range(0, 8))
        deal_weights(nc, w1_rest[:], w1_raw[0], slice(1, PACK), range(0, 8))
        deal_weights(nc, w1_first[:], w1_raw[1], slice(0, 1), range(8, 16))
        for t in range(1, PACK):
            deal_weights(nc, w1_rest[:, t - 1 : t], w1_raw[1], slice(t, t + 1), range(8, 16))
        w1_codes = keep.tile([P, H], U32, name="w1_codes", tag="chain", align_bytes=ALIGN)
        w1_scale = keep.tile([P, H], U8, name="w1_scale", align_bytes=ALIGN)
        quantize(w1_codes[:, :P], w1_scale[:, :P], w1_first[:, 0].rearrange("p m j -> p (m j)"))
        late_codes = keep.tile([P, S - EARLY], U32, name="late_codes", tag="w1_first", align_bytes=ALIGN)
        nc.vector.tensor_copy(late_codes[:], words_all[:].indirect(offs_sb[:, EARLY // LIST_ROWS :]))
        for t in range(1, PACK):
            quantize(
                w1_codes[:, t * P : (t + 1) * P],
                w1_scale[:, t * P : (t + 1) * P],
                w1_rest[:, t - 1].rearrange("p m j -> p (m j)"),
            )

        y = [keep.tile([P, S], F32, name=f"y{t}") for t in range(PACK)]
        for t in range(PACK):
            acc = bank([P, HALF])
            product(acc[:], w1_codes, w1_scale, t, early_codes[:, :HALF], x_scale[:, :HALF])
            nc.scalar.copy(out=y[t][:, :HALF], in_=acc[:])
            if t == 0:
                for codes, first, last in ((early_codes[:, HALF:], HALF, EARLY), (late_codes[:], EARLY, S)):
                    acc = bank([P, last - first])
                    product(acc[:], w1_codes, w1_scale, t, codes, x_scale[:, first:last])
                    nc.vector.tensor_copy(out=y[t][:, first:last], in_=acc[:])
            else:
                acc = bank([P, HALF])
                for codes, first, last in ((early_codes[:, HALF:], HALF, EARLY), (late_codes[:], EARLY, S)):
                    product(acc[:, first - HALF : last - HALF], w1_codes, w1_scale, t, codes, x_scale[:, first:last])
                nc.scalar.copy(out=y[t][:, HALF:], in_=acc[:])

        w2_grouped = keep.tile([P, PACK, P, PACK], BF16, name="w2_grouped", tag="chain", align_bytes=ALIGN)
        deal_weights(nc, w2_grouped[:], w2_raw, slice(0, PACK), range(0, 16))
        w3_grouped = keep.tile([P, N, PACK], BF16, name="w3_grouped", align_bytes=ALIGN)
        nc.scalar.copy(out=w3_grouped[:], in_=w3_raw[:].rearrange("p j c -> p c j"))

        z = [keep.tile([P, PACK, POOLED], BF16, name=f"z{c}") for c in range(2)]
        for t in range(PACK):
            lined = [keep.tile([P, HALF], BF16, name=f"lined{t}_{c}") for c in range(2)]
            for c in range(2):
                nc.vector.tensor_copy(lined[c][:], y[t][:].indirect(n1_sb[:, c * cols : (c + 1) * cols]))
            for c in range(2):
                pairs = lined[c][:].rearrange("p (v e) -> p e v", e=2)
                nc.vector.tensor_tensor(z[c][:, t, :], pairs[:, 0], pairs[:, 1], MAX)

        w2_codes = keep.tile([P, H], U32, name="w2_codes", align_bytes=ALIGN)
        w2_scale = keep.tile([P, H], U8, name="w2_scale", align_bytes=ALIGN)
        quantize(w2_codes[:], w2_scale[:], w2_grouped[:].rearrange("p t m j -> p (t m j)"))

        h = [keep.tile([P, V], F32, name=f"h{t}") for t in range(PACK)]
        slot_cols = POOLED // LIST_ROWS
        z_grouped = [keep.tile([P, POOLED, PACK], BF16, name=f"z_grouped{c}", align_bytes=ALIGN) for c in range(2)]
        nc.vector.tensor_copy(out=z_grouped[0][:], in_=z[0][:].rearrange("p t v -> p v t"))
        nc.scalar.copy(out=z_grouped[1][:], in_=z[1][:].rearrange("p t v -> p v t"))
        for c in range(2):
            z_codes = keep.tile(
                [P, POOLED], U32, name=f"z_codes{c}", tag=("chain" if c == 0 else "z_second"), align_bytes=ALIGN
            )
            z_scale = keep.tile([P, POOLED], U8, name=f"z_scale{c}", align_bytes=ALIGN)
            quantize(z_codes[:], z_scale[:], z_grouped[c][:].rearrange("p v t -> p (v t)"))
            for t in (1, 3, 0, 2):
                acc = bank([P, POOLED])
                product(acc[:], w2_codes, w2_scale, t, z_codes[:], z_scale[:])
                nc.scalar.copy(out=h[t][:, c * POOLED : (c + 1) * POOLED], in_=acc[:])

        w3_codes = keep.tile([P, N], U32, name="w3_codes", align_bytes=ALIGN)
        w3_scale = keep.tile([P, N], U8, name="w3_scale", align_bytes=ALIGN)
        quantize(w3_codes[:], w3_scale[:], w3_grouped[:].rearrange("p c j -> p (c j)"))

        for c in range(2):
            for t in (1, 3):
                nc.vector.tensor_copy(
                    page[t][:].indirect(n2_sb[:, c * slot_cols : (c + 1) * slot_cols]),
                    h[t][:, c * POOLED : (c + 1) * POOLED],
                )
        for t in (1, 3):
            nc.scalar.copy(out=page[t - 1][:, U:], in_=page[t][:])
        starts = [sum(PAGE_CHUNKS[:c]) for c in range(len(PAGE_CHUNKS))]
        z2_grouped = [
            keep.tile([P, width, PACK], BF16, name=f"z2_grouped{c}", align_bytes=ALIGN)
            for c, width in enumerate(PAGE_CHUNKS)
        ]

        def weave(copy, c, t):
            both = page[t][:].rearrange("p (e w) -> p w e", e=2)[:, starts[c] : starts[c] + PAGE_CHUNKS[c], :]
            copy(out=z2_grouped[c][:, :, t : t + 2], in_=both)

        nc.vector.tensor_copy(page[0][:].indirect(n2_sb[:]), h[0][:])
        for c in range(len(PAGE_CHUNKS)):
            weave(nc.scalar.copy, c, 0)
        nc.vector.tensor_copy(page[2][:].indirect(n2_sb[:]), h[2][:])

        out_rows = out.rearrange("(t p) w -> p t w", t=PACK)
        z2_mx = []
        for c, width in enumerate(PAGE_CHUNKS):
            weave(nc.vector.tensor_copy if c == 0 else nc.scalar.copy, c, 2)
            z2_codes = keep.tile([P, width], U32, name=f"z2_codes{c}", align_bytes=ALIGN)
            z2_scale = keep.tile([P, width], U8, name=f"z2_scale{c}", align_bytes=ALIGN)
            quantize(z2_codes[:], z2_scale[:], z2_grouped[c][:].rearrange("p w t -> p (w t)"))
            z2_mx.append((z2_codes, z2_scale))
        for c, width in enumerate(PAGE_CHUNKS):
            z2_codes, z2_scale = z2_mx[c]
            per_bank = BANK // width
            columns = slice(starts[c], starts[c] + width)
            for first in range(0, PACK, per_bank):
                acc = bank([P, per_bank, width])
                for t in range(first, first + per_bank):
                    product(acc[:, t - first, :], w3_codes, w3_scale, t, z2_codes[:], z2_scale[:])
                rows = slice(first, first + per_bank)
                result = keep.tile([P, per_bank, width], F32, name=f"result{c}_{first}")
                nc.vector.tensor_tensor(result[:], acc[:], res_sb[:, rows, columns], ADD)
                nc.sync.dma_start(out_rows[:, rows, columns], result[:])
